import numpy as np
import ml_dtypes

BF16 = ml_dtypes.bfloat16


def bf(x):
    return np.asarray(x, np.float32).astype(BF16)


def f32(x):
    return np.asarray(x, np.float32)


def f64(x):
    return np.asarray(x).astype(np.float64)


def striped(idx):
    return np.tile(idx.reshape(-1, 16).T, (8, 1))


S, K, M, N, E, Q = 512, 256, 256, 1024, 4, 256


def two_experts():
    first = np.random.permutation(S).reshape(E, S // E)
    return np.concatenate([np.random.permutation(np.concatenate([first[e], first[(e + 1) % E]])) for e in range(E)])


def setup_inputs():
    return {"table": bf(np.random.standard_normal((S, K))), "w": bf(np.random.standard_normal((E, K, M)) / np.sqrt(K)), "b": f32(0.5 * np.random.standard_normal((M, 1))), "offs": striped(two_experts())}


def reference(table, w, b, offs):
    idx = offs[:16].T.reshape(-1)
    x = f64(table)[idx].T
    y = np.concatenate([f64(w)[e].T @ x[:, e * Q : (e + 1) * Q] for e in range(E)], axis=1)
    return np.maximum(y + f64(b), 0.0)

@@ -1,0 +1,61 @@
+import concourse.mybir as mybir
+from concourse.masks import make_identity
+
+P = 128
+TOKENS, K, M = 512, 256, 256
+EXPERTS, PIECE = 4, 256
+KB = K // P
+MB = M // P
+TB = TOKENS // P
+LIST_COLUMNS = PIECE // 16
+
+FLOPS = 2 * EXPERTS * PIECE * K * M
+
+BF16, F32, U16 = mybir.dt.bfloat16, mybir.dt.float32, mybir.dt.uint16
+ADD, MAX = mybir.AluOpType.add, mybir.AluOpType.max
+
+
+def tile_gather_matmul_kernel(tc, table, w, b, offs, out):
+    nc = tc.nc
+    with (
+        tc.tile_pool(name="held", bufs=1) as held,
+        tc.tile_pool(name="results", bufs=8) as results,
+        tc.psum_pool(name="flip_psum", bufs=1) as flip_psum,
+        tc.psum_pool(name="sum_psum", bufs=6) as sum_psum,
+    ):
+        tokens = held.tile([P, TB, K], BF16, name="tokens")
+        offsets = held.tile([P, EXPERTS * LIST_COLUMNS], U16, name="offsets")
+        weights = held.tile([P, EXPERTS, KB, M], BF16, name="weights")
+        bias = held.tile([P, MB], F32, name="bias")
+        identity = held.tile([P, P], BF16, name="identity")
+
+        nc.sync.dma_start(tokens[:], table.rearrange("(t p) k -> p t k", p=P))
+        nc.sync.dma_start(offsets[:], offs)
+        nc.scalar.dma_start(weights[:], w.rearrange("e (c p) m -> p e c m", p=P))
+        nc.scalar.dma_start(bias[:], b.rearrange("(a p) o -> p (a o)", p=P))
+        make_identity(nc, identity[:])
+
+        flipped = []
+        for c in range(KB):
+            bank = flip_psum.tile([P, TOKENS], BF16, name=f"flip_bank{c}")
+            for t in range(TB):
+                nc.tensor.transpose(bank[:, t * P : (t + 1) * P], tokens[:, t, c * P : (c + 1) * P], identity[:])
+            window = held.tile([P, TOKENS], BF16, name=f"flipped{c}")
+            nc.vector.tensor_copy(window[:], bank[:])
+            flipped.append(window)
+
+        for e in range(EXPERTS):
+            piece = offsets[:, e * LIST_COLUMNS : (e + 1) * LIST_COLUMNS]
+            for a in range(MB):
+                total = sum_psum.tile([P, PIECE], F32, name="total")
+                for c in range(KB):
+                    nc.tensor.matmul(
+                        total[:],
+                        weights[:, e, c, a * P : (a + 1) * P],
+                        flipped[c][:].indirect(piece),
+                        start=c == 0,
+                        stop=c == KB - 1,
+                    )
+                result = results.tile([P, PIECE], F32, name="result")
+                nc.vector.tensor_scalar(result[:], total[:], bias[:, a : a + 1], 0.0, ADD, MAX)
+                nc.sync.dma_start(out[a * P : (a + 1) * P, e * PIECE : (e + 1) * PIECE], result[:])

@@ -8,6 +8,7 @@ KB = K // P
 MB = M // P
 TB = TOKENS // P
 LIST_COLUMNS = PIECE // 16
+WARM_UP = 5
 
 FLOPS = 2 * EXPERTS * PIECE * K * M
 
@@ -21,8 +22,15 @@ def tile_gather_matmul_kernel(tc, table, w, b, offs, out):
         tc.tile_pool(name="held", bufs=1) as held,
         tc.tile_pool(name="results", bufs=8) as results,
         tc.psum_pool(name="flip_psum", bufs=1) as flip_psum,
-        tc.psum_pool(name="sum_psum", bufs=6) as sum_psum,
+        tc.psum_pool(name="warm_psum", bufs=1) as warm_psum,
+        tc.psum_pool(name="sum_psum", bufs=5) as sum_psum,
     ):
+        zeros = held.tile([P, 512], BF16, name="zeros")
+        nc.vector.memset(zeros[:], 0.0)
+        unread = warm_psum.tile([P, 512], F32, name="unread")
+        for step in range(WARM_UP):
+            nc.tensor.matmul(unread[:], zeros[:, :P], zeros[:], start=True, stop=True)
+
         tokens = held.tile([P, TB, K], BF16, name="tokens")
         offsets = held.tile([P, EXPERTS * LIST_COLUMNS], U16, name="offsets")
         weights = held.tile([P, EXPERTS, KB, M], BF16, name="weights")
@@ -31,7 +39,9 @@ def tile_gather_matmul_kernel(tc, table, w, b, offs, out):
 
         nc.sync.dma_start(tokens[:], table.rearrange("(t p) k -> p t k", p=P))
         nc.sync.dma_start(offsets[:], offs)
-        nc.scalar.dma_start(weights[:], w.rearrange("e (c p) m -> p e c m", p=P))
+        for first in range(0, EXPERTS, 2):
+            pair = slice(first, first + 2)
+            nc.sync.dma_start(weights[:, pair], w[pair].rearrange("e (c p) m -> p e c m", p=P))
         nc.scalar.dma_start(bias[:], b.rearrange("(a p) o -> p (a o)", p=P))
         make_identity(nc, identity[:])
 

@@ -8,7 +8,7 @@ KB = K // P
 MB = M // P
 TB = TOKENS // P
 LIST_COLUMNS = PIECE // 16
-WARM_UP = 5
+WARM_UP = 4
 
 FLOPS = 2 * EXPERTS * PIECE * K * M
 
@@ -42,7 +42,7 @@ def tile_gather_matmul_kernel(tc, table, w, b, offs, out):
         for first in range(0, EXPERTS, 2):
             pair = slice(first, first + 2)
             nc.sync.dma_start(weights[:, pair], w[pair].rearrange("e (c p) m -> p e c m", p=P))
-        nc.scalar.dma_start(bias[:], b.rearrange("(a p) o -> p (a o)", p=P))
+        nc.sync.dma_start(bias[:], b.rearrange("(a p) o -> p (a o)", p=P))
         make_identity(nc, identity[:])
 
         flipped = []

@@ -7,6 +7,7 @@ EXPERTS, PIECE = 4, 256
 KB = K // P
 MB = M // P
 TB = TOKENS // P
+HALF = TOKENS // 2
 LIST_COLUMNS = PIECE // 16
 WARM_UP = 4
 
@@ -22,12 +23,11 @@ def tile_gather_matmul_kernel(tc, table, w, b, offs, out):
         tc.tile_pool(name="held", bufs=1) as held,
         tc.tile_pool(name="results", bufs=8) as results,
         tc.psum_pool(name="flip_psum", bufs=1) as flip_psum,
-        tc.psum_pool(name="warm_psum", bufs=1) as warm_psum,
-        tc.psum_pool(name="sum_psum", bufs=5) as sum_psum,
+        tc.psum_pool(name="sum_psum", bufs=4) as sum_psum,
     ):
         zeros = held.tile([P, 512], BF16, name="zeros")
         nc.vector.memset(zeros[:], 0.0)
-        unread = warm_psum.tile([P, 512], F32, name="unread")
+        unread = sum_psum.tile([P, 512], F32, name="unread", tag="total")
         for step in range(WARM_UP):
             nc.tensor.matmul(unread[:], zeros[:, :P], zeros[:], start=True, stop=True)
 
@@ -37,7 +37,9 @@ def tile_gather_matmul_kernel(tc, table, w, b, offs, out):
         bias = held.tile([P, MB], F32, name="bias")
         identity = held.tile([P, P], BF16, name="identity")
 
-        nc.sync.dma_start(tokens[:], table.rearrange("(t p) k -> p t k", p=P))
+        for h in range(2):
+            blocks = slice(h * TB // 2, (h + 1) * TB // 2)
+            nc.sync.dma_start(tokens[:, blocks], table[h * HALF : (h + 1) * HALF].rearrange("(t p) k -> p t k", p=P))
         nc.sync.dma_start(offsets[:], offs)
         for first in range(0, EXPERTS, 2):
             pair = slice(first, first + 2)
@@ -45,14 +47,14 @@ def tile_gather_matmul_kernel(tc, table, w, b, offs, out):
         nc.sync.dma_start(bias[:], b.rearrange("(a p) o -> p (a o)", p=P))
         make_identity(nc, identity[:])
 
-        flipped = []
-        for c in range(KB):
-            bank = flip_psum.tile([P, TOKENS], BF16, name=f"flip_bank{c}")
-            for t in range(TB):
-                nc.tensor.transpose(bank[:, t * P : (t + 1) * P], tokens[:, t, c * P : (c + 1) * P], identity[:])
-            window = held.tile([P, TOKENS], BF16, name=f"flipped{c}")
-            nc.vector.tensor_copy(window[:], bank[:])
-            flipped.append(window)
+        flipped = [held.tile([P, TOKENS], BF16, name=f"flipped{c}") for c in range(KB)]
+        for h in range(2):
+            for c in range(KB):
+                bank = flip_psum.tile([P, HALF], BF16, name=f"flip_bank{h}{c}")
+                for i in range(TB // 2):
+                    t = h * TB // 2 + i
+                    nc.tensor.transpose(bank[:, i * P : (i + 1) * P], tokens[:, t, c * P : (c + 1) * P], identity[:])
+                nc.vector.tensor_copy(flipped[c][:, h * HALF : (h + 1) * HALF], bank[:])
 
         for e in range(EXPERTS):
             piece = offsets[:, e * LIST_COLUMNS : (e + 1) * LIST_COLUMNS]

@@ -9,7 +9,6 @@ MB = M // P
 TB = TOKENS // P
 HALF = TOKENS // 2
 LIST_COLUMNS = PIECE // 16
-WARM_UP = 4
 
 FLOPS = 2 * EXPERTS * PIECE * K * M
 
@@ -25,12 +24,6 @@ def tile_gather_matmul_kernel(tc, table, w, b, offs, out):
         tc.psum_pool(name="flip_psum", bufs=1) as flip_psum,
         tc.psum_pool(name="sum_psum", bufs=4) as sum_psum,
     ):
-        zeros = held.tile([P, 512], BF16, name="zeros")
-        nc.vector.memset(zeros[:], 0.0)
-        unread = sum_psum.tile([P, 512], F32, name="unread", tag="total")
-        for step in range(WARM_UP):
-            nc.tensor.matmul(unread[:], zeros[:, :P], zeros[:], start=True, stop=True)
-
         tokens = held.tile([P, TB, K], BF16, name="tokens")
         offsets = held.tile([P, EXPERTS * LIST_COLUMNS], U16, name="offsets")
         weights = held.tile([P, EXPERTS, KB, M], BF16, name="weights")

import concourse.mybir as mybir
from concourse.masks import make_identity

P = 128
TOKENS, K, M = 512, 256, 256
EXPERTS, PIECE = 4, 256
KB = K // P
MB = M // P
TB = TOKENS // P
HALF = TOKENS // 2
LIST_COLUMNS = PIECE // 16

FLOPS = 2 * EXPERTS * PIECE * K * M

BF16, F32, U16 = mybir.dt.bfloat16, mybir.dt.float32, mybir.dt.uint16
ADD, MAX = mybir.AluOpType.add, mybir.AluOpType.max


def tile_gather_matmul_kernel(tc, table, w, b, offs, out):
    nc = tc.nc
    with (
        tc.tile_pool(name="held", bufs=1) as held,
        tc.tile_pool(name="results", bufs=8) as results,
        tc.psum_pool(name="flip_psum", bufs=1) as flip_psum,
        tc.psum_pool(name="sum_psum", bufs=4) as sum_psum,
    ):
        tokens = held.tile([P, TB, K], BF16, name="tokens")
        offsets = held.tile([P, EXPERTS * LIST_COLUMNS], U16, name="offsets")
        weights = held.tile([P, EXPERTS, KB, M], BF16, name="weights")
        bias = held.tile([P, MB], F32, name="bias")
        identity = held.tile([P, P], BF16, name="identity")

        for h in range(2):
            blocks = slice(h * TB // 2, (h + 1) * TB // 2)
            nc.sync.dma_start(tokens[:, blocks], table[h * HALF : (h + 1) * HALF].rearrange("(t p) k -> p t k", p=P))
        nc.sync.dma_start(offsets[:], offs)
        for first in range(0, EXPERTS, 2):
            pair = slice(first, first + 2)
            nc.sync.dma_start(weights[:, pair], w[pair].rearrange("e (c p) m -> p e c m", p=P))
        nc.sync.dma_start(bias[:], b.rearrange("(a p) o -> p (a o)", p=P))
        make_identity(nc, identity[:])

        flipped = [held.tile([P, TOKENS], BF16, name=f"flipped{c}") for c in range(KB)]
        for h in range(2):
            for c in range(KB):
                bank = flip_psum.tile([P, HALF], BF16, name=f"flip_bank{h}{c}")
                for i in range(TB // 2):
                    t = h * TB // 2 + i
                    nc.tensor.transpose(bank[:, i * P : (i + 1) * P], tokens[:, t, c * P : (c + 1) * P], identity[:])
                nc.vector.tensor_copy(flipped[c][:, h * HALF : (h + 1) * HALF], bank[:])

        for e in range(EXPERTS):
            piece = offsets[:, e * LIST_COLUMNS : (e + 1) * LIST_COLUMNS]
            for a in range(MB):
                total = sum_psum.tile([P, PIECE], F32, name="total")
                for c in range(KB):
                    nc.tensor.matmul(
                        total[:],
                        weights[:, e, c, a * P : (a + 1) * P],
                        flipped[c][:].indirect(piece),
                        start=c == 0,
                        stop=c == KB - 1,
                    )
                result = results.tile([P, PIECE], F32, name="result")
                nc.vector.tensor_scalar(result[:], total[:], bias[:, a : a + 1], 0.0, ADD, MAX)
                nc.sync.dma_start(out[a * P : (a + 1) * P, e * PIECE : (e + 1) * PIECE], result[:])
